import numpy as np
import ml_dtypes


def mxq(x, axis, fmt="e4m3"):
    dtype, down = {"e4m3": (ml_dtypes.float8_e4m3fn, 7), "e5m2": (ml_dtypes.float8_e5m2, 14)}[fmt]
    v = np.moveaxis(np.asarray(x, np.float32).astype(ml_dtypes.bfloat16).astype(np.float64), axis, -1)
    blocks = v.reshape(v.shape[:-1] + (-1, 32))
    amax = np.abs(blocks).max(-1, keepdims=True)
    byte = np.maximum(np.where(amax > 0, np.frexp(amax)[1] - 1 + 127, 0) - down, 1)
    scale = np.exp2(byte - 127.0)
    codes = (blocks / scale).astype(np.float32).astype(dtype).astype(np.float64)
    return np.moveaxis((codes * scale).reshape(v.shape), -1, axis)


WIDE = False


def mx_kscale(k):
    if not WIDE:
        return np.ones(k)
    levels = np.array([10, -10, 5, -5, 0])
    if k % 512:
        return np.exp2(np.random.permutation(np.resize(levels, k // 32))).repeat(32)
    a = np.empty((k // 512, 16))
    for p in range(k // 512):
        a[p, :8] = np.random.permutation(np.resize(levels, 8))
        for g in range(8):
            far = levels[np.abs(levels - a[p, g]) >= 10]
            a[p, g + 8] = far[np.random.randint(len(far))]
    return np.exp2(a.ravel()).repeat(32)


def f64(x):
    return np.asarray(x).astype(np.float64)


def striped(idx):
    return np.tile(np.asarray(idx).reshape(-1, 16).T, (8, 1)).astype(np.uint16)


def unstriped(offs):
    return offs[:16].T.reshape(-1).astype(np.int64)


E2M1 = np.array([0.0, 0.5, 1.0, 1.5, 2.0, 3.0, 4.0, 6.0, -0.0, -0.5, -1.0, -1.5, -2.0, -3.0, -4.0, -6.0])


def pack_weight(w, fmt):
    k, n = w.shape
    w = f64(np.asarray(w, np.float32).astype(ml_dtypes.bfloat16)).reshape(k // 32, 32, n)
    amax = np.abs(w).max(1)
    if fmt == "e4m3":
        byte = np.frexp(amax)[1] - 1 + 127 - 7
    else:
        mant, ex = np.frexp(amax / 6.0)
        byte = np.where(mant > 0.5, ex, ex - 1) + 127
    byte = np.clip(np.where(amax > 0, byte, 1), 1, 254)
    scaled = (w * np.exp2(127.0 - byte)[:, None, :]).reshape(k, n).astype(np.float32)
    by_word = np.ascontiguousarray(scaled.reshape(k // 512, 128, 4, n).transpose(0, 1, 3, 2))
    if fmt == "e4m3":
        words = by_word.astype(ml_dtypes.float8_e4m3fn).view(np.uint8)
    else:
        c = by_word.astype(ml_dtypes.float4_e2m1fn).view(np.uint8) & 0xF
        words = (c[..., 0::2] | (c[..., 1::2] << 4)).reshape(k // 512, 128, 2 * n)
    return np.ascontiguousarray(words), np.ascontiguousarray(byte.astype(np.uint8).reshape(k // 512, 16, n))


def unpack_weight(words, scales, fmt):
    g, _, n = scales.shape
    words = np.ascontiguousarray(words).reshape(g, 128, n, -1)
    if fmt == "e4m3":
        vals = words.view(ml_dtypes.float8_e4m3fn).astype(np.float64)
    else:
        nib = np.empty((g, 128, n, 4), np.uint8)
        nib[..., 0::2] = words & 0xF
        nib[..., 1::2] = words >> 4
        vals = E2M1[nib]
    vals = vals * np.repeat(np.exp2(scales.astype(np.float64) - 127.0), 8, axis=1)[..., None]
    return vals.transpose(0, 1, 3, 2).reshape(g * 512, n)


D, E, T, I, Q = 512, 512, 2048, 512, 128


def setup_inputs():
    n = np.random.standard_normal
    idx = np.random.permutation(T)[:I]
    fd = mx_kscale(D)
    fe = mx_kscale(E)
    keysp = pack_weight(n((D, T)) / fd[:, None], "e2m1")
    valsp = pack_weight(n((E, T)) / fe[:, None], "e2m1")
    return {
        "query": (n((D, Q)) * 0.8 / np.sqrt(D) * fd[:, None]).astype(np.float32),
        "query2": (n((D, Q)) * 0.8 / np.sqrt(D) * fd[:, None]).astype(np.float32),
        "query3": (n((D, Q)) * 0.8 / np.sqrt(D) * fd[:, None]).astype(np.float32),
        "keys_words": keysp[0],
        "keys_scales": keysp[1],
        "gout": (n((E, Q)) * 1 / np.sqrt(E) * fe[:, None]).astype(np.float32),
        "vals_words": valsp[0],
        "vals_scales": valsp[1],
        "size": (np.random.uniform(0.5, 2.0, (1, I))).astype(np.float32),
        "old": (0.5 * n((Q, T))).astype(np.float32),
        "offs": striped(idx),
    }


def reference(query, query2, query3, keys_words, keys_scales, gout, vals_words, vals_scales, size, old, offs):
    idx = unstriped(offs)
    keysu = unpack_weight(keys_words, keys_scales, "e2m1")
    valsu = unpack_weight(vals_words, vals_scales, "e2m1")
    queryq = mxq(f64(query), 0, "e4m3")
    keysidxg = keysu[:, idx]
    a = queryq.T @ keysidxg
    query2q = mxq(f64(query2), 0, "e4m3")
    b = query2q.T @ keysidxg
    query3q = mxq(f64(query3), 0, "e4m3")
    h1 = query3q.T @ keysidxg
    s = np.log(np.exp(a) + np.exp(b) + np.exp(h1))
    p = np.exp(s - np.max(s, axis=1, keepdims=True))
    z = np.sum(p, axis=1, keepdims=True)
    goutq = mxq(f64(gout), 0, "e4m3")
    valsidxg = valsu[:, idx]
    c0 = goutq.T @ valsidxg
    dz = np.sum(c0 * p * f64(size) / np.square(z) * (-1.0), axis=1, keepdims=True)
    dp = c0 / z * f64(size) + dz
    ds = dp * p
    da = ds / (np.exp(a) + np.exp(b) + np.exp(h1)) * np.exp(a)
    gs = da * 512.0
    gf = np.zeros((Q, T))
    gf[:, idx] = gs
    y = f64(old) + gf
    return y

@@ -1,0 +1,177 @@
+from contextlib import ExitStack
+
+import concourse.mybir as mybir
+from concourse.masks import make_identity
+
+D, E, T, SLOTS, Q = 512, 512, 2048, 512, 128
+FLOPS = 2 * Q * SLOTS * (3 * D + E)
+
+F32 = mybir.dt.float32
+BF16 = mybir.dt.bfloat16
+I32 = mybir.dt.int32
+U32 = mybir.dt.uint32
+U16 = mybir.dt.uint16
+U8 = mybir.dt.uint8
+FP8X4 = mybir.dt.float8_e4m3fn_x4
+FP4X4 = mybir.dt.float4_e2m1fn_x4
+ALU = mybir.AluOpType
+ACT = mybir.ActivationFunctionType
+AX = mybir.AxisListType
+
+P = 128
+PACK = 4
+GAIN = 512.0
+OUT_CHUNK = 512
+
+
+def tile_attend_bcommittee_s_kernel(tc, query, query2, query3, keys_words, keys_scales, gout,
+                                     vals_words, vals_scales, size, old, offs, out):
+    nc = tc.nc
+    with ExitStack() as ctx:
+        keep = ctx.enter_context(tc.tile_pool(name="keep", bufs=1))
+        psum = ctx.enter_context(tc.psum_pool(name="psum", bufs=1))
+
+        def load_words(name, words):
+            pool_words = keep.tile([P, T], U16, name=name, tag="pool_words", align_bytes=64)
+            nc.sync.dma_start(out=pool_words[:].bitcast(I32), in_=words[0].bitcast(I32))
+            return pool_words
+
+        def load_scales(name, scales):
+            pool_scales = keep.tile([P, T], U8, name=name, tag=name, align_bytes=64)
+            nc.gpsimd.memset(pool_scales[:].bitcast(I32), 0)
+            for quad in range(4):
+                nc.sync.dma_start(out=pool_scales[32 * quad:32 * quad + 4, :].bitcast(I32),
+                                  in_=scales[0, 4 * quad:4 * quad + 4, :].bitcast(I32))
+            return pool_scales
+
+        def load_rows(name, tag, rows):
+            raw = keep.tile([P, PACK, Q], F32, name=name, tag=tag, align_bytes=64)
+            nc.sync.dma_start(out=raw[:], in_=rows.rearrange("(p j) w -> p j w", j=PACK))
+            return raw
+
+        def load_old(n, tag):
+            chunk = keep.tile([Q, OUT_CHUNK], F32, name="old%d" % n, tag=tag, align_bytes=64)
+            nc.sync.dma_start(out=chunk[:], in_=old[:, n * OUT_CHUNK:(n + 1) * OUT_CHUNK])
+            return chunk
+
+        def gather(name, tag, pool_tile, dtype):
+            picked = keep.tile([P, SLOTS], dtype, name=name, tag=tag, align_bytes=64)
+            nc.vector.tensor_copy(out=picked[:], in_=pool_tile[:].indirect(offsets[:]))
+            return picked
+
+        def interleave(name, raw):
+            grouped = keep.tile([P, Q, PACK], BF16, name=name + "_bf16", tag=name + "_bf16", align_bytes=64)
+            nc.scalar.copy(out=grouped[:].rearrange("p (c i) t -> p c t i", i=4),
+                           in_=raw[:].rearrange("p t (c i) -> p c t i", i=4))
+            return grouped
+
+        def quantise(name, grouped):
+            codes = keep.tile([P, Q], U32, name=name + "_codes", tag=name + "_codes", align_bytes=64)
+            scales = keep.tile([P, Q], U8, name=name + "_scales", align_bytes=64)
+            nc.vector.quantize_mx(out=codes[:].bitcast(FP8X4), scales=scales[:],
+                                  in_=grouped[:].rearrange("p w j -> p (w j)"))
+            return codes, scales
+
+        def product(name, rows, words, scales):
+            acc = psum.tile([Q, SLOTS], F32, name=name)
+            nc.tensor.matmul_mx(out=acc[:], lhsT=rows[0][:].bitcast(FP8X4), lhsT_scale=rows[1][:],
+                                rhs=words[:].bitcast(FP4X4), rhs_scale=scales[:], start=True, stop=True)
+            return acc
+
+        def negate_and_bound(name, score, low_before):
+            negated = keep.tile([Q, SLOTS], F32, name=name + "_negated")
+            low = keep.tile([Q, 1], F32, name=name + "_low")
+            nc.vector.tensor_scalar(out=negated[:], in0=score[:], scalar1=-1.0, scalar2=low_before,
+                                    op0=ALU.mult, op1=ALU.min, accum_out=low[:])
+            return negated, low
+
+        def exponential(name, negated, low):
+            e = keep.tile([Q, SLOTS], F32, name=name + "_exp")
+            total = keep.tile([Q, 1], F32, name=name + "_sum")
+            nc.scalar.activation(out=e[:], in_=negated[:], func=ACT.Exp, bias=low[:], scale=-1.0, accum_out=total[:])
+            return e, total
+
+        offsets = keep.tile([P, SLOTS // 16], U16, name="offsets")
+        nc.sync.dma_start(offsets[:], offs)
+        key_words = load_words("key_words", keys_words)
+        key_scales = load_scales("key_scales", keys_scales)
+        raw_a = load_rows("raw_a", "stage0", query)
+        raw_b = load_rows("raw_b", "stage1", query2)
+        raw_h = load_rows("raw_h", "stage2", query3)
+        val_scales = load_scales("val_scales", vals_scales)
+        size_cols = keep.tile([P, PACK], F32, name="size_cols")
+        nc.sync.dma_start(out=size_cols[:], in_=size.rearrange("o (p c) -> (o p) c", c=PACK))
+
+        window = keep.tile([Q, T], F32, name="window")
+        nc.vector.memset(window[:].bitcast(I32), 0)
+        ident = keep.tile([P, P], F32, name="ident")
+        make_identity(nc, ident[:])
+
+        picked_key_scales = gather("picked_key_scales", "picked_key_scales", key_scales, U8)
+        picked_key_words = gather("picked_key_words", "picked_key_words", key_words, U16)
+        grouped_a = interleave("a", raw_a)
+        raw_g = load_rows("raw_g", "stage0", gout)
+        val_words = load_words("val_words", vals_words)
+        score_a = product("score_a", quantise("a", grouped_a), picked_key_words, picked_key_scales)
+        score_b = product("score_b", quantise("b", interleave("b", raw_b)), picked_key_words, picked_key_scales)
+        picked_val_scales = gather("picked_val_scales", "picked_val_scales", val_scales, U8)
+        score_h = product("score_h", quantise("h", interleave("h", raw_h)), picked_key_words, picked_key_scales)
+        grouped_g = interleave("g", raw_g)
+        old_chunks = [load_old(n, tag) for n, tag in enumerate(("stage1", "stage2", "val_scales", "stage0"))]
+
+        size_turned = psum.tile([P, PACK, P], F32, name="size_turned")
+        for c in range(PACK):
+            nc.tensor.transpose(size_turned[:, c, :], size_cols[:, c:c + 1].to_broadcast([P, P]), ident[:])
+        size_rows = keep.tile([Q, SLOTS], F32, name="size_rows", tag="h_bf16", align_bytes=64)
+        nc.scalar.copy(out=size_rows[:].rearrange("m (p c) -> m p c", c=PACK),
+                       in_=size_turned[:].rearrange("m c p -> m p c"))
+
+        neg_a, low_a = negate_and_bound("a", score_a, None)
+        rows_g = quantise("g", grouped_g)
+        neg_b, low_ab = negate_and_bound("b", score_b, low_a[:])
+        exp_a, sum_a = exponential("a", neg_a, low_ab)
+        exp_b, sum_b = exponential("b", neg_b, low_ab)
+        exp_ab = keep.tile([Q, SLOTS], F32, name="exp_ab")
+        nc.gpsimd.tensor_tensor(out=exp_ab[:], in0=exp_a[:], in1=exp_b[:], op=ALU.add)
+        sum_ab = keep.tile([Q, 1], F32, name="sum_ab")
+        nc.scalar.activation(out=sum_ab[:], in_=sum_a[:], func=ACT.Identity, bias=sum_b[:], scale=1.0)
+
+        picked_val_words = gather("picked_val_words", "h_codes", val_words, U16)
+        c0 = product("c0", rows_g, picked_val_words, picked_val_scales)
+
+        neg_h, low = negate_and_bound("h", score_h, low_ab[:])
+        shrink = keep.tile([Q, 1], F32, name="shrink")
+        nc.scalar.activation(out=shrink[:], in_=low_ab[:], func=ACT.Exp, bias=low[:], scale=-1.0)
+        exp_h, sum_h = exponential("h", neg_h, low)
+        z = keep.tile([Q, 1], F32, name="z")
+        nc.scalar.activation(out=z[:], in_=sum_ab[:], func=ACT.Identity, bias=sum_h[:], scale=shrink[:])
+        gain = keep.tile([Q, 1], F32, name="gain")
+        nc.scalar.activation(out=gain[:], in_=shrink[:], func=ACT.Copy, scale=GAIN)
+
+        u = keep.tile([Q, SLOTS], F32, name="u")
+        nc.vector.tensor_tensor(out=u[:], in0=c0[:], in1=size_rows[:], op=ALU.mult)
+        dots = keep.tile([Q, 2], F32, name="dots")
+        weighted_ab = keep.tile([Q, SLOTS], F32, name="weighted_ab")
+        nc.vector.scalar_tensor_tensor(out=weighted_ab[:], in0=exp_ab[:], scalar=shrink[:], in1=u[:],
+                                       op0=ALU.mult, op1=ALU.mult, accum_out=dots[:, 0:1])
+        inv_z = keep.tile([Q, 1], F32, name="inv_z")
+        nc.vector.reciprocal(out=inv_z[:], in_=z[:])
+        weighted_h = keep.tile([Q, SLOTS], F32, name="weighted_h")
+        nc.vector.scalar_tensor_tensor(out=weighted_h[:], in0=exp_h[:], scalar=1.0, in1=u[:],
+                                       op0=ALU.mult, op1=ALU.mult, accum_out=dots[:, 1:2])
+        dot_parts = keep.tile([Q, 2], F32, name="dot_parts")
+        mean_u = keep.tile([Q, 1], F32, name="mean_u")
+        nc.vector.tensor_scalar(out=dot_parts[:], in0=dots[:], scalar1=inv_z[:], scalar2=None,
+                                op0=ALU.mult, op1=ALU.add, accum_out=mean_u[:])
+        centred = keep.tile([Q, SLOTS], F32, name="centred")
+        nc.vector.tensor_scalar(out=centred[:], in0=u[:], scalar1=mean_u[:], scalar2=inv_z[:],
+                                op0=ALU.subtract, op1=ALU.mult)
+        nc.vector.tensor_tensor(out=window[:].indirect(offsets[:]), in0=centred[:], in1=exp_a[:], op=ALU.mult)
+
+        pieces = [(n, 0, OUT_CHUNK) for n in range(3)] + [(3, 0, OUT_CHUNK // 2), (3, OUT_CHUNK // 2, OUT_CHUNK)]
+        for n, lo, hi in pieces:
+            cols = slice(n * OUT_CHUNK + lo, n * OUT_CHUNK + hi)
+            result = keep.tile([Q, hi - lo], F32, name="result%d_%d" % (n, lo))
+            nc.vector.scalar_tensor_tensor(out=result[:], in0=window[:, cols], scalar=gain[:], in1=old_chunks[n][:, lo:hi],
+                                           op0=ALU.mult, op1=ALU.add)
+            nc.sync.dma_start(out=out[:, cols], in_=result[:])

@@ -21,7 +21,8 @@ AX = mybir.AxisListType
 P = 128
 PACK = 4
 GAIN = 512.0
-OUT_CHUNK = 512
+OUT_WIDTHS = (256, 512, 512, 512, 256)
+OUT_STARTS = tuple(sum(OUT_WIDTHS[:n]) for n in range(len(OUT_WIDTHS)))
 
 
 def tile_attend_bcommittee_s_kernel(tc, query, query2, query3, keys_words, keys_scales, gout,
@@ -32,7 +33,7 @@ def tile_attend_bcommittee_s_kernel(tc, query, query2, query3, keys_words, keys_
         psum = ctx.enter_context(tc.psum_pool(name="psum", bufs=1))
 
         def load_words(name, words):
-            pool_words = keep.tile([P, T], U16, name=name, tag="pool_words", align_bytes=64)
+            pool_words = keep.tile([P, T], U16, name=name, tag=name, align_bytes=64)
             nc.sync.dma_start(out=pool_words[:].bitcast(I32), in_=words[0].bitcast(I32))
             return pool_words
 
@@ -49,9 +50,9 @@ def tile_attend_bcommittee_s_kernel(tc, query, query2, query3, keys_words, keys_
             nc.sync.dma_start(out=raw[:], in_=rows.rearrange("(p j) w -> p j w", j=PACK))
             return raw
 
-        def load_old(n, tag):
-            chunk = keep.tile([Q, OUT_CHUNK], F32, name="old%d" % n, tag=tag, align_bytes=64)
-            nc.sync.dma_start(out=chunk[:], in_=old[:, n * OUT_CHUNK:(n + 1) * OUT_CHUNK])
+        def load_old(n):
+            chunk = keep.tile([Q, OUT_WIDTHS[n]], F32, name="old%d" % n)
+            nc.sync.dma_start(out=chunk[:], in_=old[:, OUT_STARTS[n]:OUT_STARTS[n] + OUT_WIDTHS[n]])
             return chunk
 
         def gather(name, tag, pool_tile, dtype):
@@ -59,28 +60,30 @@ def tile_attend_bcommittee_s_kernel(tc, query, query2, query3, keys_words, keys_
             nc.vector.tensor_copy(out=picked[:], in_=pool_tile[:].indirect(offsets[:]))
             return picked
 
-        def interleave(name, raw):
-            grouped = keep.tile([P, Q, PACK], BF16, name=name + "_bf16", tag=name + "_bf16", align_bytes=64)
-            nc.scalar.copy(out=grouped[:].rearrange("p (c i) t -> p c t i", i=4),
-                           in_=raw[:].rearrange("p t (c i) -> p c t i", i=4))
+        def interleave(name, raws):
+            grouped = keep.tile([P, len(raws) * Q, PACK], BF16, name=name + "_bf16", tag=name + "_bf16", align_bytes=64)
+            for n, raw in enumerate(raws):
+                nc.scalar.copy(out=grouped[:, n * Q:(n + 1) * Q, :].rearrange("p (c i) t -> p c t i", i=4),
+                               in_=raw[:].rearrange("p t (c i) -> p c t i", i=4))
             return grouped
 
         def quantise(name, grouped):
-            codes = keep.tile([P, Q], U32, name=name + "_codes", tag=name + "_codes", align_bytes=64)
-            scales = keep.tile([P, Q], U8, name=name + "_scales", align_bytes=64)
+            width = grouped.shape[1]
+            codes = keep.tile([P, width], U32, name=name + "_codes", align_bytes=64)
+            scales = keep.tile([P, width], U8, name=name + "_scales", align_bytes=64)
             nc.vector.quantize_mx(out=codes[:].bitcast(FP8X4), scales=scales[:],
                                   in_=grouped[:].rearrange("p w j -> p (w j)"))
-            return codes, scales
+            return [(codes[:, lo:lo + Q], scales[:, lo:lo + Q]) for lo in range(0, width, Q)]
 
         def product(name, rows, words, scales):
             acc = psum.tile([Q, SLOTS], F32, name=name)
-            nc.tensor.matmul_mx(out=acc[:], lhsT=rows[0][:].bitcast(FP8X4), lhsT_scale=rows[1][:],
+            nc.tensor.matmul_mx(out=acc[:], lhsT=rows[0].bitcast(FP8X4), lhsT_scale=rows[1],
                                 rhs=words[:].bitcast(FP4X4), rhs_scale=scales[:], start=True, stop=True)
             return acc
 
-        def negate_and_bound(name, score, low_before):
-            negated = keep.tile([Q, SLOTS], F32, name=name + "_negated")
-            low = keep.tile([Q, 1], F32, name=name + "_low")
+        def negate_and_bound(name, score, low_before, tag):
+            negated = keep.tile([Q, SLOTS], F32, name=name + "_negated", tag=tag, align_bytes=64)
+            low = keep.tile([Q, 1], F32, name=name + "_low", tag=name + "_low", align_bytes=64)
             nc.vector.tensor_scalar(out=negated[:], in0=score[:], scalar1=-1.0, scalar2=low_before,
                                     op0=ALU.mult, op1=ALU.min, accum_out=low[:])
             return negated, low
@@ -94,13 +97,16 @@ def tile_attend_bcommittee_s_kernel(tc, query, query2, query3, keys_words, keys_
         offsets = keep.tile([P, SLOTS // 16], U16, name="offsets")
         nc.sync.dma_start(offsets[:], offs)
         key_words = load_words("key_words", keys_words)
+        size_cols = keep.tile([P, PACK], F32, name="size_cols")
+        nc.sync.dma_start(out=size_cols[:], in_=size.rearrange("o (p c) -> (o p) c", c=PACK))
         key_scales = load_scales("key_scales", keys_scales)
         raw_a = load_rows("raw_a", "stage0", query)
         raw_b = load_rows("raw_b", "stage1", query2)
         raw_h = load_rows("raw_h", "stage2", query3)
         val_scales = load_scales("val_scales", vals_scales)
-        size_cols = keep.tile([P, PACK], F32, name="size_cols")
-        nc.sync.dma_start(out=size_cols[:], in_=size.rearrange("o (p c) -> (o p) c", c=PACK))
+        raw_g = load_rows("raw_g", "stage3", gout)
+        val_words = load_words("val_words", vals_words)
+        old_chunks = [load_old(n) for n in range(len(OUT_WIDTHS))]
 
         window = keep.tile([Q, T], F32, name="window")
         nc.vector.memset(window[:].bitcast(I32), 0)
@@ -109,15 +115,12 @@ def tile_attend_bcommittee_s_kernel(tc, query, query2, query3, keys_words, keys_
 
         picked_key_scales = gather("picked_key_scales", "picked_key_scales", key_scales, U8)
         picked_key_words = gather("picked_key_words", "picked_key_words", key_words, U16)
-        grouped_a = interleave("a", raw_a)
-        raw_g = load_rows("raw_g", "stage0", gout)
-        val_words = load_words("val_words", vals_words)
-        score_a = product("score_a", quantise("a", grouped_a), picked_key_words, picked_key_scales)
-        score_b = product("score_b", quantise("b", interleave("b", raw_b)), picked_key_words, picked_key_scales)
+        rows_a, rows_b = quantise("ab", interleave("ab", [raw_a, raw_b]))
+        score_a = product("score_a", rows_a, picked_key_words, picked_key_scales)
+        score_b = product("score_b", rows_b, picked_key_words, picked_key_scales)
         picked_val_scales = gather("picked_val_scales", "picked_val_scales", val_scales, U8)
-        score_h = product("score_h", quantise("h", interleave("h", raw_h)), picked_key_words, picked_key_scales)
-        grouped_g = interleave("g", raw_g)
-        old_chunks = [load_old(n, tag) for n, tag in enumerate(("stage1", "stage2", "val_scales", "stage0"))]
+        score_h = product("score_h", quantise("h", interleave("h", [raw_h]))[0], picked_key_words, picked_key_scales)
+        grouped_g = interleave("g", [raw_g])
 
         size_turned = psum.tile([P, PACK, P], F32, name="size_turned")
         for c in range(PACK):
@@ -126,9 +129,9 @@ def tile_attend_bcommittee_s_kernel(tc, query, query2, query3, keys_words, keys_
         nc.scalar.copy(out=size_rows[:].rearrange("m (p c) -> m p c", c=PACK),
                        in_=size_turned[:].rearrange("m c p -> m p c"))
 
-        neg_a, low_a = negate_and_bound("a", score_a, None)
-        rows_g = quantise("g", grouped_g)
-        neg_b, low_ab = negate_and_bound("b", score_b, low_a[:])
+        neg_a, low_a = negate_and_bound("a", score_a, None, "neg_a")
+        rows_g = quantise("g", grouped_g)[0]
+        neg_b, low_ab = negate_and_bound("b", score_b, low_a[:], "neg_b")
         exp_a, sum_a = exponential("a", neg_a, low_ab)
         exp_b, sum_b = exponential("b", neg_b, low_ab)
         exp_ab = keep.tile([Q, SLOTS], F32, name="exp_ab")
@@ -136,42 +139,45 @@ def tile_attend_bcommittee_s_kernel(tc, query, query2, query3, keys_words, keys_
         sum_ab = keep.tile([Q, 1], F32, name="sum_ab")
         nc.scalar.activation(out=sum_ab[:], in_=sum_a[:], func=ACT.Identity, bias=sum_b[:], scale=1.0)
 
-        picked_val_words = gather("picked_val_words", "h_codes", val_words, U16)
+        picked_val_words = gather("picked_val_words", "a_low", val_words, U16)
         c0 = product("c0", rows_g, picked_val_words, picked_val_scales)
 
-        neg_h, low = negate_and_bound("h", score_h, low_ab[:])
+        neg_h, low = negate_and_bound("h", score_h, low_ab[:], "val_words")
         shrink = keep.tile([Q, 1], F32, name="shrink")
         nc.scalar.activation(out=shrink[:], in_=low_ab[:], func=ACT.Exp, bias=low[:], scale=-1.0)
         exp_h, sum_h = exponential("h", neg_h, low)
         z = keep.tile([Q, 1], F32, name="z")
         nc.scalar.activation(out=z[:], in_=sum_ab[:], func=ACT.Identity, bias=sum_h[:], scale=shrink[:])
-        gain = keep.tile([Q, 1], F32, name="gain")
-        nc.scalar.activation(out=gain[:], in_=shrink[:], func=ACT.Copy, scale=GAIN)
 
         u = keep.tile([Q, SLOTS], F32, name="u")
         nc.vector.tensor_tensor(out=u[:], in0=c0[:], in1=size_rows[:], op=ALU.mult)
-        dots = keep.tile([Q, 2], F32, name="dots")
+        scaled_u = keep.tile([Q, SLOTS], F32, name="scaled_u")
+        nc.scalar.activation(out=scaled_u[:], in_=u[:], func=ACT.Copy, scale=z[:])
+        dot_ab = keep.tile([Q, 1], F32, name="dot_ab")
         weighted_ab = keep.tile([Q, SLOTS], F32, name="weighted_ab")
         nc.vector.scalar_tensor_tensor(out=weighted_ab[:], in0=exp_ab[:], scalar=shrink[:], in1=u[:],
-                                       op0=ALU.mult, op1=ALU.mult, accum_out=dots[:, 0:1])
-        inv_z = keep.tile([Q, 1], F32, name="inv_z")
-        nc.vector.reciprocal(out=inv_z[:], in_=z[:])
+                                       op0=ALU.mult, op1=ALU.mult, accum_out=dot_ab[:])
+        dot_h = keep.tile([Q, 1], F32, name="dot_h")
         weighted_h = keep.tile([Q, SLOTS], F32, name="weighted_h")
         nc.vector.scalar_tensor_tensor(out=weighted_h[:], in0=exp_h[:], scalar=1.0, in1=u[:],
-                                       op0=ALU.mult, op1=ALU.mult, accum_out=dots[:, 1:2])
-        dot_parts = keep.tile([Q, 2], F32, name="dot_parts")
-        mean_u = keep.tile([Q, 1], F32, name="mean_u")
-        nc.vector.tensor_scalar(out=dot_parts[:], in0=dots[:], scalar1=inv_z[:], scalar2=None,
-                                op0=ALU.mult, op1=ALU.add, accum_out=mean_u[:])
+                                       op0=ALU.mult, op1=ALU.mult, accum_out=dot_h[:])
         centred = keep.tile([Q, SLOTS], F32, name="centred")
-        nc.vector.tensor_scalar(out=centred[:], in0=u[:], scalar1=mean_u[:], scalar2=inv_z[:],
-                                op0=ALU.subtract, op1=ALU.mult)
+        nc.vector.tensor_scalar(out=centred[:], in0=scaled_u[:], scalar1=dot_ab[:], scalar2=dot_h[:],
+                                op0=ALU.subtract, op1=ALU.subtract)
+        inv_z = keep.tile([Q, 1], F32, name="inv_z")
+        nc.vector.reciprocal(out=inv_z[:], in_=z[:])
         nc.vector.tensor_tensor(out=window[:].indirect(offsets[:]), in0=centred[:], in1=exp_a[:], op=ALU.mult)
 
-        pieces = [(n, 0, OUT_CHUNK) for n in range(3)] + [(3, 0, OUT_CHUNK // 2), (3, OUT_CHUNK // 2, OUT_CHUNK)]
-        for n, lo, hi in pieces:
-            cols = slice(n * OUT_CHUNK + lo, n * OUT_CHUNK + hi)
-            result = keep.tile([Q, hi - lo], F32, name="result%d_%d" % (n, lo))
-            nc.vector.scalar_tensor_tensor(out=result[:], in0=window[:, cols], scalar=gain[:], in1=old_chunks[n][:, lo:hi],
+        share = keep.tile([Q, 1], F32, name="share")
+        nc.scalar.activation(out=share[:], in_=inv_z[:], func=ACT.Copy, scale=shrink[:])
+        share_over_z = keep.tile([Q, 1], F32, name="share_over_z")
+        nc.scalar.activation(out=share_over_z[:], in_=share[:], func=ACT.Copy, scale=inv_z[:])
+        gain = keep.tile([Q, 1], F32, name="gain")
+        nc.scalar.activation(out=gain[:], in_=share_over_z[:], func=ACT.Copy, scale=GAIN)
+
+        for n, width in enumerate(OUT_WIDTHS):
+            cols = slice(OUT_STARTS[n], OUT_STARTS[n] + width)
+            result = keep.tile([Q, width], F32, name="result%d" % n)
+            nc.vector.scalar_tensor_tensor(out=result[:], in0=window[:, cols], scalar=gain[:], in1=old_chunks[n][:],
                                            op0=ALU.mult, op1=ALU.add)
             nc.sync.dma_start(out=out[:, cols], in_=result[:])

@@ -97,13 +97,13 @@ def tile_attend_bcommittee_s_kernel(tc, query, query2, query3, keys_words, keys_
         offsets = keep.tile([P, SLOTS // 16], U16, name="offsets")
         nc.sync.dma_start(offsets[:], offs)
         key_words = load_words("key_words", keys_words)
-        size_cols = keep.tile([P, PACK], F32, name="size_cols")
-        nc.sync.dma_start(out=size_cols[:], in_=size.rearrange("o (p c) -> (o p) c", c=PACK))
         key_scales = load_scales("key_scales", keys_scales)
         raw_a = load_rows("raw_a", "stage0", query)
         raw_b = load_rows("raw_b", "stage1", query2)
         raw_h = load_rows("raw_h", "stage2", query3)
         val_scales = load_scales("val_scales", vals_scales)
+        size_cols = keep.tile([P, PACK], F32, name="size_cols")
+        nc.gpsimd.dma_start(out=size_cols[:], in_=size.rearrange("o (p c) -> (o p) c", c=PACK))
         raw_g = load_rows("raw_g", "stage3", gout)
         val_words = load_words("val_words", vals_words)
         old_chunks = [load_old(n) for n in range(len(OUT_WIDTHS))]
@@ -139,8 +139,14 @@ def tile_attend_bcommittee_s_kernel(tc, query, query2, query3, keys_words, keys_
         sum_ab = keep.tile([Q, 1], F32, name="sum_ab")
         nc.scalar.activation(out=sum_ab[:], in_=sum_a[:], func=ACT.Identity, bias=sum_b[:], scale=1.0)
 
-        picked_val_words = gather("picked_val_words", "a_low", val_words, U16)
-        c0 = product("c0", rows_g, picked_val_words, picked_val_scales)
+        picked_val_words = keep.tile([P, SLOTS], U16, name="picked_val_words", tag="a_low", align_bytes=64)
+        c0 = psum.tile([Q, SLOTS], F32, name="c0")
+        for lo in range(0, SLOTS, SLOTS // 2):
+            hi = lo + SLOTS // 2
+            nc.vector.tensor_copy(out=picked_val_words[:, lo:hi], in_=val_words[:].indirect(offsets[:, lo // 16:hi // 16]))
+            nc.tensor.matmul_mx(out=c0[:, lo:hi], lhsT=rows_g[0].bitcast(FP8X4), lhsT_scale=rows_g[1],
+                                rhs=picked_val_words[:, lo:hi].bitcast(FP4X4), rhs_scale=picked_val_scales[:, lo:hi],
+                                start=True, stop=True)
 
         neg_h, low = negate_and_bound("h", score_h, low_ab[:], "val_words")
         shrink = keep.tile([Q, 1], F32, name="shrink")

@@ -37,12 +37,11 @@ def tile_attend_bcommittee_s_kernel(tc, query, query2, query3, keys_words, keys_
             nc.sync.dma_start(out=pool_words[:].bitcast(I32), in_=words[0].bitcast(I32))
             return pool_words
 
-        def load_scales(name, scales):
+        def load_scales(name, scales, clearing_engine):
             pool_scales = keep.tile([P, T], U8, name=name, tag=name, align_bytes=64)
-            nc.gpsimd.memset(pool_scales[:].bitcast(I32), 0)
-            for quad in range(4):
-                nc.sync.dma_start(out=pool_scales[32 * quad:32 * quad + 4, :].bitcast(I32),
-                                  in_=scales[0, 4 * quad:4 * quad + 4, :].bitcast(I32))
+            clearing_engine.memset(pool_scales[:].bitcast(I32), 0)
+            for r in range(4):
+                nc.sync.dma_start(out=pool_scales[r:P:32, :].bitcast(I32), in_=scales[0, r:16:4, :].bitcast(I32))
             return pool_scales
 
         def load_rows(name, tag, rows):
@@ -97,11 +96,11 @@ def tile_attend_bcommittee_s_kernel(tc, query, query2, query3, keys_words, keys_
         offsets = keep.tile([P, SLOTS // 16], U16, name="offsets")
         nc.sync.dma_start(offsets[:], offs)
         key_words = load_words("key_words", keys_words)
-        key_scales = load_scales("key_scales", keys_scales)
+        key_scales = load_scales("key_scales", keys_scales, nc.vector)
         raw_a = load_rows("raw_a", "stage0", query)
         raw_b = load_rows("raw_b", "stage1", query2)
+        val_scales = load_scales("val_scales", vals_scales, nc.gpsimd)
         raw_h = load_rows("raw_h", "stage2", query3)
-        val_scales = load_scales("val_scales", vals_scales)
         size_cols = keep.tile([P, PACK], F32, name="size_cols")
         nc.gpsimd.dma_start(out=size_cols[:], in_=size.rearrange("o (p c) -> (o p) c", c=PACK))
         raw_g = load_rows("raw_g", "stage3", gout)

from contextlib import ExitStack

import concourse.mybir as mybir
from concourse.masks import make_identity

D, E, T, SLOTS, Q = 512, 512, 2048, 512, 128
FLOPS = 2 * Q * SLOTS * (3 * D + E)

F32 = mybir.dt.float32
BF16 = mybir.dt.bfloat16
I32 = mybir.dt.int32
U32 = mybir.dt.uint32
U16 = mybir.dt.uint16
U8 = mybir.dt.uint8
FP8X4 = mybir.dt.float8_e4m3fn_x4
FP4X4 = mybir.dt.float4_e2m1fn_x4
ALU = mybir.AluOpType
ACT = mybir.ActivationFunctionType
AX = mybir.AxisListType

P = 128
PACK = 4
GAIN = 512.0
OUT_WIDTHS = (256, 512, 512, 512, 256)
OUT_STARTS = tuple(sum(OUT_WIDTHS[:n]) for n in range(len(OUT_WIDTHS)))


def tile_attend_bcommittee_s_kernel(tc, query, query2, query3, keys_words, keys_scales, gout,
                                     vals_words, vals_scales, size, old, offs, out):
    nc = tc.nc
    with ExitStack() as ctx:
        keep = ctx.enter_context(tc.tile_pool(name="keep", bufs=1))
        psum = ctx.enter_context(tc.psum_pool(name="psum", bufs=1))

        def load_words(name, words):
            pool_words = keep.tile([P, T], U16, name=name, tag=name, align_bytes=64)
            nc.sync.dma_start(out=pool_words[:].bitcast(I32), in_=words[0].bitcast(I32))
            return pool_words

        def load_scales(name, scales, clearing_engine):
            pool_scales = keep.tile([P, T], U8, name=name, tag=name, align_bytes=64)
            clearing_engine.memset(pool_scales[:].bitcast(I32), 0)
            for r in range(4):
                nc.sync.dma_start(out=pool_scales[r:P:32, :].bitcast(I32), in_=scales[0, r:16:4, :].bitcast(I32))
            return pool_scales

        def load_rows(name, tag, rows):
            raw = keep.tile([P, PACK, Q], F32, name=name, tag=tag, align_bytes=64)
            nc.sync.dma_start(out=raw[:], in_=rows.rearrange("(p j) w -> p j w", j=PACK))
            return raw

        def load_old(n):
            chunk = keep.tile([Q, OUT_WIDTHS[n]], F32, name="old%d" % n)
            nc.sync.dma_start(out=chunk[:], in_=old[:, OUT_STARTS[n]:OUT_STARTS[n] + OUT_WIDTHS[n]])
            return chunk

        def gather(name, tag, pool_tile, dtype):
            picked = keep.tile([P, SLOTS], dtype, name=name, tag=tag, align_bytes=64)
            nc.vector.tensor_copy(out=picked[:], in_=pool_tile[:].indirect(offsets[:]))
            return picked

        def interleave(name, raws):
            grouped = keep.tile([P, len(raws) * Q, PACK], BF16, name=name + "_bf16", tag=name + "_bf16", align_bytes=64)
            for n, raw in enumerate(raws):
                nc.scalar.copy(out=grouped[:, n * Q:(n + 1) * Q, :].rearrange("p (c i) t -> p c t i", i=4),
                               in_=raw[:].rearrange("p t (c i) -> p c t i", i=4))
            return grouped

        def quantise(name, grouped):
            width = grouped.shape[1]
            codes = keep.tile([P, width], U32, name=name + "_codes", align_bytes=64)
            scales = keep.tile([P, width], U8, name=name + "_scales", align_bytes=64)
            nc.vector.quantize_mx(out=codes[:].bitcast(FP8X4), scales=scales[:],
                                  in_=grouped[:].rearrange("p w j -> p (w j)"))
            return [(codes[:, lo:lo + Q], scales[:, lo:lo + Q]) for lo in range(0, width, Q)]

        def product(name, rows, words, scales):
            acc = psum.tile([Q, SLOTS], F32, name=name)
            nc.tensor.matmul_mx(out=acc[:], lhsT=rows[0].bitcast(FP8X4), lhsT_scale=rows[1],
                                rhs=words[:].bitcast(FP4X4), rhs_scale=scales[:], start=True, stop=True)
            return acc

        def negate_and_bound(name, score, low_before, tag):
            negated = keep.tile([Q, SLOTS], F32, name=name + "_negated", tag=tag, align_bytes=64)
            low = keep.tile([Q, 1], F32, name=name + "_low", tag=name + "_low", align_bytes=64)
            nc.vector.tensor_scalar(out=negated[:], in0=score[:], scalar1=-1.0, scalar2=low_before,
                                    op0=ALU.mult, op1=ALU.min, accum_out=low[:])
            return negated, low

        def exponential(name, negated, low):
            e = keep.tile([Q, SLOTS], F32, name=name + "_exp")
            total = keep.tile([Q, 1], F32, name=name + "_sum")
            nc.scalar.activation(out=e[:], in_=negated[:], func=ACT.Exp, bias=low[:], scale=-1.0, accum_out=total[:])
            return e, total

        offsets = keep.tile([P, SLOTS // 16], U16, name="offsets")
        nc.sync.dma_start(offsets[:], offs)
        key_words = load_words("key_words", keys_words)
        key_scales = load_scales("key_scales", keys_scales, nc.vector)
        raw_a = load_rows("raw_a", "stage0", query)
        raw_b = load_rows("raw_b", "stage1", query2)
        val_scales = load_scales("val_scales", vals_scales, nc.gpsimd)
        raw_h = load_rows("raw_h", "stage2", query3)
        size_cols = keep.tile([P, PACK], F32, name="size_cols")
        nc.gpsimd.dma_start(out=size_cols[:], in_=size.rearrange("o (p c) -> (o p) c", c=PACK))
        raw_g = load_rows("raw_g", "stage3", gout)
        val_words = load_words("val_words", vals_words)
        old_chunks = [load_old(n) for n in range(len(OUT_WIDTHS))]

        window = keep.tile([Q, T], F32, name="window")
        nc.vector.memset(window[:].bitcast(I32), 0)
        ident = keep.tile([P, P], F32, name="ident")
        make_identity(nc, ident[:])

        picked_key_scales = gather("picked_key_scales", "picked_key_scales", key_scales, U8)
        picked_key_words = gather("picked_key_words", "picked_key_words", key_words, U16)
        rows_a, rows_b = quantise("ab", interleave("ab", [raw_a, raw_b]))
        score_a = product("score_a", rows_a, picked_key_words, picked_key_scales)
        score_b = product("score_b", rows_b, picked_key_words, picked_key_scales)
        picked_val_scales = gather("picked_val_scales", "picked_val_scales", val_scales, U8)
        score_h = product("score_h", quantise("h", interleave("h", [raw_h]))[0], picked_key_words, picked_key_scales)
        grouped_g = interleave("g", [raw_g])

        size_turned = psum.tile([P, PACK, P], F32, name="size_turned")
        for c in range(PACK):
            nc.tensor.transpose(size_turned[:, c, :], size_cols[:, c:c + 1].to_broadcast([P, P]), ident[:])
        size_rows = keep.tile([Q, SLOTS], F32, name="size_rows", tag="h_bf16", align_bytes=64)
        nc.scalar.copy(out=size_rows[:].rearrange("m (p c) -> m p c", c=PACK),
                       in_=size_turned[:].rearrange("m c p -> m p c"))

        neg_a, low_a = negate_and_bound("a", score_a, None, "neg_a")
        rows_g = quantise("g", grouped_g)[0]
        neg_b, low_ab = negate_and_bound("b", score_b, low_a[:], "neg_b")
        exp_a, sum_a = exponential("a", neg_a, low_ab)
        exp_b, sum_b = exponential("b", neg_b, low_ab)
        exp_ab = keep.tile([Q, SLOTS], F32, name="exp_ab")
        nc.gpsimd.tensor_tensor(out=exp_ab[:], in0=exp_a[:], in1=exp_b[:], op=ALU.add)
        sum_ab = keep.tile([Q, 1], F32, name="sum_ab")
        nc.scalar.activation(out=sum_ab[:], in_=sum_a[:], func=ACT.Identity, bias=sum_b[:], scale=1.0)

        picked_val_words = keep.tile([P, SLOTS], U16, name="picked_val_words", tag="a_low", align_bytes=64)
        c0 = psum.tile([Q, SLOTS], F32, name="c0")
        for lo in range(0, SLOTS, SLOTS // 2):
            hi = lo + SLOTS // 2
            nc.vector.tensor_copy(out=picked_val_words[:, lo:hi], in_=val_words[:].indirect(offsets[:, lo // 16:hi // 16]))
            nc.tensor.matmul_mx(out=c0[:, lo:hi], lhsT=rows_g[0].bitcast(FP8X4), lhsT_scale=rows_g[1],
                                rhs=picked_val_words[:, lo:hi].bitcast(FP4X4), rhs_scale=picked_val_scales[:, lo:hi],
                                start=True, stop=True)

        neg_h, low = negate_and_bound("h", score_h, low_ab[:], "val_words")
        shrink = keep.tile([Q, 1], F32, name="shrink")
        nc.scalar.activation(out=shrink[:], in_=low_ab[:], func=ACT.Exp, bias=low[:], scale=-1.0)
        exp_h, sum_h = exponential("h", neg_h, low)
        z = keep.tile([Q, 1], F32, name="z")
        nc.scalar.activation(out=z[:], in_=sum_ab[:], func=ACT.Identity, bias=sum_h[:], scale=shrink[:])

        u = keep.tile([Q, SLOTS], F32, name="u")
        nc.vector.tensor_tensor(out=u[:], in0=c0[:], in1=size_rows[:], op=ALU.mult)
        scaled_u = keep.tile([Q, SLOTS], F32, name="scaled_u")
        nc.scalar.activation(out=scaled_u[:], in_=u[:], func=ACT.Copy, scale=z[:])
        dot_ab = keep.tile([Q, 1], F32, name="dot_ab")
        weighted_ab = keep.tile([Q, SLOTS], F32, name="weighted_ab")
        nc.vector.scalar_tensor_tensor(out=weighted_ab[:], in0=exp_ab[:], scalar=shrink[:], in1=u[:],
                                       op0=ALU.mult, op1=ALU.mult, accum_out=dot_ab[:])
        dot_h = keep.tile([Q, 1], F32, name="dot_h")
        weighted_h = keep.tile([Q, SLOTS], F32, name="weighted_h")
        nc.vector.scalar_tensor_tensor(out=weighted_h[:], in0=exp_h[:], scalar=1.0, in1=u[:],
                                       op0=ALU.mult, op1=ALU.mult, accum_out=dot_h[:])
        centred = keep.tile([Q, SLOTS], F32, name="centred")
        nc.vector.tensor_scalar(out=centred[:], in0=scaled_u[:], scalar1=dot_ab[:], scalar2=dot_h[:],
                                op0=ALU.subtract, op1=ALU.subtract)
        inv_z = keep.tile([Q, 1], F32, name="inv_z")
        nc.vector.reciprocal(out=inv_z[:], in_=z[:])
        nc.vector.tensor_tensor(out=window[:].indirect(offsets[:]), in0=centred[:], in1=exp_a[:], op=ALU.mult)

        share = keep.tile([Q, 1], F32, name="share")
        nc.scalar.activation(out=share[:], in_=inv_z[:], func=ACT.Copy, scale=shrink[:])
        share_over_z = keep.tile([Q, 1], F32, name="share_over_z")
        nc.scalar.activation(out=share_over_z[:], in_=share[:], func=ACT.Copy, scale=inv_z[:])
        gain = keep.tile([Q, 1], F32, name="gain")
        nc.scalar.activation(out=gain[:], in_=share_over_z[:], func=ACT.Copy, scale=GAIN)

        for n, width in enumerate(OUT_WIDTHS):
            cols = slice(OUT_STARTS[n], OUT_STARTS[n] + width)
            result = keep.tile([Q, width], F32, name="result%d" % n)
            nc.vector.scalar_tensor_tensor(out=result[:], in0=window[:, cols], scalar=gain[:], in1=old_chunks[n][:],
                                           op0=ALU.mult, op1=ALU.add)
            nc.sync.dma_start(out=out[:, cols], in_=result[:])
